import numpy as np
import ml_dtypes


def mxq(x, axis, fmt="e4m3"):
    dtype, down = {"e4m3": (ml_dtypes.float8_e4m3fn, 7), "e5m2": (ml_dtypes.float8_e5m2, 14)}[fmt]
    v = np.moveaxis(np.asarray(x, np.float32).astype(ml_dtypes.bfloat16).astype(np.float64), axis, -1)
    blocks = v.reshape(v.shape[:-1] + (-1, 32))
    amax = np.abs(blocks).max(-1, keepdims=True)
    byte = np.maximum(np.where(amax > 0, np.frexp(amax)[1] - 1 + 127, 0) - down, 1)
    scale = np.exp2(byte - 127.0)
    codes = (blocks / scale).astype(np.float32).astype(dtype).astype(np.float64)
    return np.moveaxis((codes * scale).reshape(v.shape), -1, axis)


WIDE = False


def mx_kscale(k):
    if not WIDE:
        return np.ones(k)
    levels = np.array([10, -10, 5, -5, 0])
    if k % 512:
        return np.exp2(np.random.permutation(np.resize(levels, k // 32))).repeat(32)
    a = np.empty((k // 512, 16))
    for p in range(k // 512):
        a[p, :8] = np.random.permutation(np.resize(levels, 8))
        for g in range(8):
            far = levels[np.abs(levels - a[p, g]) >= 10]
            a[p, g + 8] = far[np.random.randint(len(far))]
    return np.exp2(a.ravel()).repeat(32)


def f64(x):
    return np.asarray(x).astype(np.float64)


def striped(idx):
    return np.tile(idx.reshape(-1, 16).T, (8, 1)).astype(np.uint16)


def unstriped(offs):
    return offs[:16].T.reshape(-1).astype(np.int64)


E2M1 = np.array([0.0, 0.5, 1.0, 1.5, 2.0, 3.0, 4.0, 6.0, -0.0, -0.5, -1.0, -1.5, -2.0, -3.0, -4.0, -6.0])


def pack_weight(w, fmt):
    k, n = w.shape
    w = f64(np.asarray(w, np.float32).astype(ml_dtypes.bfloat16)).reshape(k // 32, 32, n)
    amax = np.abs(w).max(1)
    if fmt == "e4m3":
        byte = np.frexp(amax)[1] - 1 + 127 - 7
    else:
        mant, ex = np.frexp(amax / 6.0)
        byte = np.where(mant > 0.5, ex, ex - 1) + 127
    byte = np.clip(np.where(amax > 0, byte, 1), 1, 254)
    scaled = (w * np.exp2(127.0 - byte)[:, None, :]).reshape(k, n).astype(np.float32)
    by_word = np.ascontiguousarray(scaled.reshape(k // 512, 128, 4, n).transpose(0, 1, 3, 2))
    if fmt == "e4m3":
        words = by_word.astype(ml_dtypes.float8_e4m3fn).view(np.uint8)
    else:
        c = by_word.astype(ml_dtypes.float4_e2m1fn).view(np.uint8) & 0xF
        words = (c[..., 0::2] | (c[..., 1::2] << 4)).reshape(k // 512, 128, 2 * n)
    return np.ascontiguousarray(words), np.ascontiguousarray(byte.astype(np.uint8).reshape(k // 512, 16, n))


def unpack_weight(words, scales, fmt):
    g, _, n = scales.shape
    words = np.ascontiguousarray(words).reshape(g, 128, n, -1)
    if fmt == "e4m3":
        vals = words.view(ml_dtypes.float8_e4m3fn).astype(np.float64)
    else:
        nib = np.empty((g, 128, n, 4), np.uint8)
        nib[..., 0::2] = words & 0xF
        nib[..., 1::2] = words >> 4
        vals = E2M1[nib]
    vals = vals * np.repeat(np.exp2(scales.astype(np.float64) - 127.0), 8, axis=1)[..., None]
    return vals.transpose(0, 1, 3, 2).reshape(g * 512, n)


def gelu(v):
    return 0.5 * v * (1.0 + np.tanh(np.sqrt(2.0 / np.pi) * (v + 0.044715 * v**3)))


def bf(x):
    return np.asarray(x, np.float32).astype(ml_dtypes.bfloat16)


def planes(Y):
    n, m = Y.shape
    b = f64(bf(Y)).reshape(n // 32, 32, m)
    amax = np.abs(b).max(1)
    byte = np.clip(np.where(amax > 0, np.frexp(amax)[1] - 1 + 127 - 7, 1), 1, 254)
    codes = (b * np.exp2(127.0 - byte)[:, None, :]).reshape(n, m).astype(np.float32).astype(ml_dtypes.float8_e4m3fn).view(np.uint8)
    words = codes.reshape(n // 512, 128, 4, m).transpose(0, 1, 3, 2)
    return np.ascontiguousarray(words), np.ascontiguousarray(byte.astype(np.uint8).reshape(n // 512, 16, m))


K, H, N, T, S, K2, T2, P = 1024, 1024, 512, 4096, 1024, 512, 2048, 512

def setup_inputs():
    n = np.random.standard_normal
    s = mx_kscale(K)[:, None]
    s2 = mx_kscale(K2)[:, None]
    u = mx_kscale(H)[:, None]
    tab_words, tab_scales = pack_weight(n((K, T)) * s, "e4m3")
    tab2_words, tab2_scales = pack_weight(n((K2, T2)) * s2, "e4m3")
    w2_words, w2_scales = pack_weight(0.8 * n((H, N)) / np.sqrt(H) / u, "e2m1")
    return {
        "tab_words": tab_words, "tab_scales": tab_scales,
        "offs": striped(np.random.permutation(T)[:S]),
        "tab2_words": tab2_words, "tab2_scales": tab2_scales,
        "offs2": striped(np.random.permutation(T2)[:P]),
        "pos1": striped(np.random.permutation(S)[:P]),
        "w1": (0.38 * n((K, H)) / np.sqrt(K) / s).astype(np.float32),
        "b1": np.random.uniform(-1.0, 1.0, H).astype(np.float32),
        "gh": (np.exp(0.3 * n(H)) * u[:, 0]).astype(np.float32),
        "w2_words": w2_words, "w2_scales": w2_scales,
        "w3": (n((K2, N)) / np.sqrt(K2) / s2).astype(np.float32),
        "tol": np.exp(0.8 * n(N)).astype(np.float32),
    }

def reference(tab_words, tab_scales, offs, tab2_words, tab2_scales, offs2, pos1, w1, b1, gh, w2_words, w2_scales, w3, tol):
    v = unpack_weight(tab_words, tab_scales, "e4m3")[:, unstriped(offs)]
    v2 = unpack_weight(tab2_words, tab2_scales, "e4m3")[:, unstriped(offs2)]
    w2 = unpack_weight(w2_words, w2_scales, "e2m1")
    a = (mxq(f64(w1), 0, "e4m3").T @ v) + f64(b1)[:, None]
    h = f64(gh)[:, None] * (a + np.sin(a))
    d = w2.T @ mxq(h, 0, "e4m3")
    b = mxq(f64(w3), 0, "e4m3").T @ v2
    y = f64(tol)[:, None] * np.minimum(d[:, unstriped(pos1)], b)
    words, scales = planes(y)
    return y, words, scales

@@ -1,0 +1,267 @@
+from contextlib import ExitStack
+
+import concourse.mybir as mybir
+
+K, H, N, T, S, K2, T2, R = 1024, 1024, 512, 4096, 1024, 512, 2048, 512
+FLOPS = 2 * (K * H * S + H * N * S + K2 * N * R)
+
+F32 = mybir.dt.float32
+BF16 = mybir.dt.bfloat16
+I32 = mybir.dt.int32
+U32 = mybir.dt.uint32
+U16 = mybir.dt.uint16
+U8 = mybir.dt.uint8
+FP8X4 = mybir.dt.float8_e4m3fn_x4
+FP4X4 = mybir.dt.float4_e2m1fn_x4
+ACT = mybir.ActivationFunctionType
+ALU = mybir.AluOpType
+
+P = 128
+PACK = 4
+KP = P * PACK
+RUN = 4
+H_GROUPS = [(0, 0, 512, "x"), (0, 512, 512, "x"), (1, 0, 512, "x"), (1, 512, 256, "x"), (1, 768, 256, "a")]
+Y_CHUNKS = [(0, 384), (384, 128)]
+
+
+def tile_list_session_tolerance_bound_kernel(
+    tc, tab_words, tab_scales, offs, tab2_words, tab2_scales, offs2, pos1, w1, b1, gh, w2_words, w2_scales, w3, tol,
+    out_0, out_1, out_2,
+):
+    nc = tc.nc
+    with ExitStack() as ctx:
+        keep = ctx.enter_context(tc.tile_pool(name="keep", bufs=1))
+        ring = ctx.enter_context(tc.tile_pool(name="ring", bufs=2))
+        sring = ctx.enter_context(tc.tile_pool(name="sring", bufs=4))
+        psum = ctx.enter_context(tc.psum_pool(name="psum", bufs=4))
+
+        def held(shape, dtype, name):
+            return keep.tile(shape, dtype, name=name, align_bytes=64)
+
+        offs_sb = held([P, S // 16], U16, "offs_sb")
+        offs2_sb = held([P, R // 16], U16, "offs2_sb")
+        pos1_sb = held([P, R // 16], U16, "pos1_sb")
+        tab_w = [held([P, T], U32, "tab_w%d" % a) for a in range(2)]
+        tab_s = held([P, T], U8, "tab_s")
+        tab2_w = held([P, T2], U32, "tab2_w")
+        tab2_s = held([P, T2], U8, "tab2_s")
+        v_w = [held([P, S], U32, "v_w%d" % a) for a in range(2)]
+        v_s = held([P, S], U8, "v_s")
+        v2_s = held([P, R], U8, "v2_s")
+        w1_raw = {(b, a): held([P, PACK, KP], F32, "w1_raw%d%d" % (b, a)) for b in range(2) for a in range(2)}
+        w1_bf = {(b, a): held([P, PACK * KP], BF16, "w1_bf%d%d" % (b, a)) for b in range(2) for a in range(2)}
+        w1_w = {(b, a): held([P, KP], U32, "w1_w%d%d" % (b, a)) for b in range(2) for a in range(2)}
+        w1_s = {(b, a): held([P, KP], U8, "w1_s%d%d" % (b, a)) for b in range(2) for a in range(2)}
+        w3_raw = held([P, PACK, N], F32, "w3_raw")
+        w3_w = held([P, N], U32, "w3_w")
+        w3_s = held([P, N], U8, "w3_s")
+        w2_raw_w = held([P, 2, 2 * N], U8, "w2_raw_w")
+        w2_raw_s = held([P, 2, N], U8, "w2_raw_s")
+        w2_w = held([P, 2, 2 * N], U8, "w2_w")
+        w2_s = held([P, 2, N], U8, "w2_s")
+        b1_sb = held([P, 2, PACK], F32, "b1_sb")
+        gh_sb = held([P, 2, PACK], F32, "gh_sb")
+        gb_sb = held([P, 2, PACK], F32, "gb_sb")
+        tol_sb = held([P, PACK], F32, "tol_sb")
+        h_w = [held([P, S], U32, "h_w%d" % b) for b in range(2)]
+        h_s = [held([P, S], U8, "h_s%d" % b) for b in range(2)]
+        d_sb = [held([P, S], F32, "d_sb%d" % t) for t in range(PACK)]
+        y_w = held([P, R], U32, "y_w")
+        y_s = held([P, R], U8, "y_s")
+
+        nc.vector.memset(tab_s[:].bitcast(I32), 0)
+        nc.vector.memset(tab2_s[:].bitcast(I32), 0)
+        nc.vector.memset(w2_raw_s[:].rearrange("p a n -> p (a n)").bitcast(I32), 0)
+
+        def words(ap):
+            return ap.rearrange("p n t -> p (n t)").bitcast(I32)
+
+        def load_w1(b, a):
+            rows = w1[a * KP : (a + 1) * KP, b * KP : (b + 1) * KP]
+            nc.sync.dma_start(out=w1_raw[b, a][:], in_=rows.rearrange("(p i) c -> p i c", i=PACK))
+
+        nc.sync.dma_start(offs_sb[:], offs)
+        nc.sync.dma_start(offs2_sb[:], offs2)
+        nc.sync.dma_start(out=tab_w[0][:].bitcast(I32), in_=words(tab_words[0]))
+        for q in range(4):
+            nc.gpsimd.dma_start(
+                out=tab_s[32 * q : 32 * q + 8, :].bitcast(I32), in_=tab_scales[:, 4 * q : 4 * q + 4, :].bitcast(I32)
+            )
+        for q in range(4):
+            nc.gpsimd.dma_start(
+                out=tab2_s[32 * q : 32 * q + 4, :].bitcast(I32), in_=tab2_scales[0, 4 * q : 4 * q + 4, :].bitcast(I32)
+            )
+        for q in range(4):
+            nc.gpsimd.dma_start(
+                out=w2_raw_s[32 * q : 32 * q + 4, :, :].bitcast(I32),
+                in_=w2_scales[:, 4 * q : 4 * q + 4, :].rearrange("a r n -> r a n").bitcast(I32),
+            )
+        load_w1(0, 0)
+        load_w1(0, 1)
+        nc.sync.dma_start(out=w2_raw_w[:].bitcast(I32), in_=w2_words.rearrange("a p n -> p a n").bitcast(I32))
+        nc.sync.dma_start(out=b1_sb[:], in_=b1.rearrange("(b p t) -> p b t", b=2, t=PACK))
+        nc.sync.dma_start(out=gh_sb[:], in_=gh.rearrange("(b p t) -> p b t", b=2, t=PACK))
+        nc.sync.dma_start(out=tab_w[1][:].bitcast(I32), in_=words(tab_words[1]))
+        load_w1(1, 0)
+        load_w1(1, 1)
+        nc.sync.dma_start(out=tab2_w[:].bitcast(I32), in_=words(tab2_words[0]))
+        nc.sync.dma_start(out=w3_raw[:], in_=w3.rearrange("(p i) c -> p i c", i=PACK))
+        nc.sync.dma_start(pos1_sb[:], pos1)
+        nc.sync.dma_start(out=tol_sb[:], in_=tol.rearrange("(p t) -> p t", t=PACK))
+
+        def deal(raw, grouped):
+            src = raw[:].rearrange("p i (m t) -> p m i t", t=PACK)
+            dst = grouped[:].rearrange("p (t m i) -> p m i t", t=PACK, i=PACK)
+            for m0 in range(0, P, 32):
+                nc.scalar.copy(out=dst[:, m0 : m0 + 32], in_=src[:, m0 : m0 + 32])
+
+        def quantize(codes, scales, grouped):
+            nc.vector.quantize_mx(out=codes.bitcast(FP8X4), scales=scales, in_=grouped)
+
+        nc.vector.tensor_copy(out=v_s[:], in_=tab_s[:].indirect(offs_sb[:]))
+        nc.vector.tensor_copy(out=v_w[0][:], in_=tab_w[0][:].indirect(offs_sb[:]))
+        nc.vector.tensor_copy(out=v2_s[:], in_=tab2_s[:].indirect(offs2_sb[:]))
+        for a in range(2):
+            deal(w1_raw[0, a], w1_bf[0, a])
+            quantize(w1_w[0, a][:], w1_s[0, a][:], w1_bf[0, a][:])
+        nc.vector.tensor_copy(
+            out=w2_w[:].bitcast(U16).rearrange("p a (t m) -> p a m t", t=PACK),
+            in_=w2_raw_w[:].bitcast(U16).rearrange("p a (m t) -> p a m t", t=PACK),
+        )
+        nc.vector.tensor_tensor(out=gb_sb[:], in0=gh_sb[:], in1=b1_sb[:], op=ALU.mult)
+        for half in range(2):
+            nc.vector.tensor_copy(
+                out=v_w[1][:, 512 * half : 512 * (half + 1)], in_=tab_w[1][:].indirect(offs_sb[:, 32 * half : 32 * (half + 1)])
+            )
+
+        def first_stage(b, j0, n, road):
+            cols = slice(j0, j0 + n)
+            if road == "x":
+                planes = ring.tile([P, PACK, n], F32, name="planes", tag="planes", align_bytes=64)
+            else:
+                planes = ring.tile([P, PACK, n], BF16, name="planes", tag="planes", align_bytes=64)
+            for t in range(PACK):
+                acc = psum.tile([P, n], F32, name="acc", tag="acc")
+                m_cols = slice(P * t, P * (t + 1))
+                for a in range(2):
+                    nc.tensor.matmul_mx(
+                        out=acc[:],
+                        lhsT=w1_w[b, a][:, m_cols].bitcast(FP8X4),
+                        lhsT_scale=w1_s[b, a][:, m_cols],
+                        rhs=v_w[a][:, cols].bitcast(FP8X4),
+                        rhs_scale=v_s[4 * a :, cols],
+                        start=(a == 0),
+                        stop=(a == 1),
+                    )
+                sine = sring.tile([P, n], F32, name="sine", tag="sine")
+                nc.scalar.activation(out=sine[:], in_=acc[:], func=ACT.Sin, bias=b1_sb[:, b, t : t + 1])
+                if road == "x":
+                    nc.vector.scalar_tensor_tensor(
+                        out=planes[:, t, :], in0=acc[:], scalar=b1_sb[:, b, t : t + 1], in1=sine[:], op0=ALU.add, op1=ALU.add
+                    )
+                else:
+                    gained = sring.tile([P, n], F32, name="gained", tag="gained")
+                    nc.scalar.activation(
+                        out=gained[:], in_=acc[:], func=ACT.Identity, bias=gb_sb[:, b, t : t + 1], scale=gh_sb[:, b, t : t + 1]
+                    )
+                    nc.vector.scalar_tensor_tensor(
+                        out=planes[:, t, :], in0=sine[:], scalar=gh_sb[:, b, t : t + 1], in1=gained[:], op0=ALU.mult, op1=ALU.add
+                    )
+            grouped = ring.tile([P, n * PACK], BF16, name="h_bf", tag="h_bf", align_bytes=64)
+            src = planes[:].rearrange("p t (c i) -> p c t i", i=RUN)
+            dst = grouped[:].rearrange("p (c i t) -> p c t i", i=RUN, t=PACK)
+            if road == "x":
+                gain = gh_sb[:, b, :].unsqueeze(1).unsqueeze(3).broadcast_to([P, n // RUN, PACK, RUN])
+                nc.vector.tensor_tensor(out=dst, in0=src, in1=gain, op=ALU.mult)
+            else:
+                nc.vector.tensor_copy(out=dst, in_=src)
+            return grouped
+
+        def second_stage(j0, n):
+            cols = slice(j0, j0 + n)
+            for t in range(PACK):
+                dacc = psum.tile([P, n], F32, name="dacc", tag="dacc")
+                for b in range(2):
+                    nc.tensor.matmul_mx(
+                        out=dacc[:],
+                        lhsT=w2_w[:, b, 2 * P * t : 2 * P * (t + 1)].bitcast(FP4X4),
+                        lhsT_scale=w2_s[:, b, P * t : P * (t + 1)],
+                        rhs=h_w[b][:, cols].bitcast(FP8X4),
+                        rhs_scale=h_s[b][:, cols],
+                        start=(b == 0),
+                        stop=(b == 1),
+                    )
+                nc.scalar.copy(out=d_sb[t][:, cols], in_=dacc[:])
+
+        for g, (b, j0, n, road) in enumerate(H_GROUPS):
+            grouped = first_stage(b, j0, n, road)
+            quantize(h_w[b][:, j0 : j0 + n], h_s[b][:, j0 : j0 + n], grouped[:])
+            if g == 1:
+                deal(w1_raw[1, 0], w1_bf[1, 0])
+                quantize(w1_w[1, 0][:], w1_s[1, 0][:], w1_bf[1, 0][:])
+                deal(w1_raw[1, 1], w1_bf[1, 1])
+                quantize(w1_w[1, 1][:], w1_s[1, 1][:], w1_bf[1, 1][:])
+                nc.vector.tensor_copy(
+                    out=w2_s[:].rearrange("p a (t m) -> p a m t", t=PACK),
+                    in_=w2_raw_s[:].rearrange("p a (m t) -> p a m t", t=PACK),
+                )
+            if g > 0 and H_GROUPS[g - 1][0] == 1:
+                second_stage(*H_GROUPS[g - 1][1:3])
+        second_stage(*H_GROUPS[-1][1:3])
+
+        w3_bf = ring.tile([P, PACK * N], BF16, name="w3_bf", tag="h_bf", align_bytes=64)
+        deal(w3_raw, w3_bf)
+        v2_w = ring.tile([P, R], U32, name="v2_w", tag="h_bf", align_bytes=64)
+        nc.vector.tensor_copy(out=v2_w[:], in_=tab2_w[:].indirect(offs2_sb[:]))
+
+        picked = {}
+
+        def pick(j0, n):
+            for t in range(PACK):
+                picked[j0, t] = held([P, n], F32, "picked%d_%d" % (j0, t))
+                nc.vector.tensor_copy(out=picked[j0, t][:], in_=d_sb[t][:].indirect(pos1_sb[:, j0 // 16 : (j0 + n) // 16]))
+
+        pick(*Y_CHUNKS[0])
+        quantize(w3_w[:], w3_s[:], w3_bf[:])
+        b_acc = []
+        for t in range(PACK):
+            acc = psum.tile([P, R], F32, name="acc", tag="acc")
+            m_cols = slice(P * t, P * (t + 1))
+            nc.tensor.matmul_mx(
+                out=acc[:],
+                lhsT=w3_w[:, m_cols].bitcast(FP8X4),
+                lhsT_scale=w3_s[:, m_cols],
+                rhs=v2_w[:].bitcast(FP8X4),
+                rhs_scale=v2_s[:],
+                start=True,
+                stop=True,
+            )
+            b_acc.append(acc)
+        pick(*Y_CHUNKS[1])
+
+        out_rows = out_0.rearrange("(p t) j -> p t j", t=PACK)
+        out_words = words(out_1[0])
+        y_bf = {}
+        y = {}
+        for j0, n in Y_CHUNKS:
+            cols = slice(j0, j0 + n)
+            y[j0] = held([P, PACK, n], F32, "y%d" % j0)
+            for t in range(PACK):
+                lower = sring.tile([P, n], F32, name="lower", tag="gained")
+                nc.vector.tensor_tensor(out=lower[:], in0=picked[j0, t][:], in1=b_acc[t][:, cols], op=ALU.min)
+                nc.scalar.activation(out=y[j0][:, t, :], in_=lower[:], func=ACT.Copy, scale=tol_sb[:, t : t + 1])
+            nc.sync.dma_start(out=out_rows[:, :, cols], in_=y[j0][:])
+            y_bf[j0] = held([P, n * PACK], BF16, "y_bf%d" % j0)
+        for j0, n in Y_CHUNKS:
+            cols = slice(j0, j0 + n)
+            src = y[j0][:].rearrange("p t (c i) -> p c t i", i=RUN)
+            dst = y_bf[j0][:].rearrange("p (c i t) -> p c t i", i=RUN, t=PACK)
+            if j0 == 0:
+                nc.scalar.copy(out=dst, in_=src)
+            else:
+                nc.vector.tensor_copy(out=dst, in_=src)
+            quantize(y_w[:, cols], y_s[:, cols], y_bf[j0][:])
+            nc.sync.dma_start(out=out_words[:, cols], in_=y_w[:, cols].bitcast(I32))
+        for q in range(4):
+            queue = nc.scalar if q % 2 else nc.sync
+            queue.dma_start(out=out_2[0, 4 * q : 4 * q + 4, :].bitcast(I32), in_=y_s[32 * q : 32 * q + 4, :].bitcast(I32))

@@ -20,7 +20,10 @@ P = 128
 PACK = 4
 KP = P * PACK
 RUN = 4
-H_GROUPS = [(0, 0, 512, "x"), (0, 512, 512, "x"), (1, 0, 512, "x"), (1, 512, 256, "x"), (1, 768, 256, "a")]
+SINES = 16384
+TAB1 = 32768
+SCALES = 49152
+H_GROUPS = [(0, 0, 512, "x"), (0, 512, 512, "x"), (1, 0, 512, "x"), (1, 512, 256, "a"), (1, 768, 256, "a")]
 Y_CHUNKS = [(0, 384), (384, 128)]
 
 
@@ -33,32 +36,29 @@ def tile_list_session_tolerance_bound_kernel(
         keep = ctx.enter_context(tc.tile_pool(name="keep", bufs=1))
         ring = ctx.enter_context(tc.tile_pool(name="ring", bufs=2))
         sring = ctx.enter_context(tc.tile_pool(name="sring", bufs=4))
+        shared = ctx.enter_context(tc.tile_pool(name="shared", bufs=1))
         psum = ctx.enter_context(tc.psum_pool(name="psum", bufs=4))
 
         def held(shape, dtype, name):
-            return keep.tile(shape, dtype, name=name, align_bytes=64)
+            return keep.tile(shape, dtype, name=name, tag=name, align_bytes=64)
 
         offs_sb = held([P, S // 16], U16, "offs_sb")
         offs2_sb = held([P, R // 16], U16, "offs2_sb")
         pos1_sb = held([P, R // 16], U16, "pos1_sb")
-        tab_w = [held([P, T], U32, "tab_w%d" % a) for a in range(2)]
-        tab_s = held([P, T], U8, "tab_s")
-        tab2_w = held([P, T2], U32, "tab2_w")
-        tab2_s = held([P, T2], U8, "tab2_s")
+        def placed(shape, dtype, name, offset, tag=None):
+            return shared.tile(shape, dtype, name=name, tag=tag or name, align_bytes=64, offset=offset)
+
+        tab_w = [None, None]
+        tab_w[0] = placed([P, T], U32, "tab_w0", 0)
+        tab_s = placed([P, T], U8, "tab_s", SCALES)
         v_w = [held([P, S], U32, "v_w%d" % a) for a in range(2)]
-        v_s = held([P, S], U8, "v_s")
-        v2_s = held([P, R], U8, "v2_s")
-        w1_raw = {(b, a): held([P, PACK, KP], F32, "w1_raw%d%d" % (b, a)) for b in range(2) for a in range(2)}
-        w1_bf = {(b, a): held([P, PACK * KP], BF16, "w1_bf%d%d" % (b, a)) for b in range(2) for a in range(2)}
-        w1_w = {(b, a): held([P, KP], U32, "w1_w%d%d" % (b, a)) for b in range(2) for a in range(2)}
+        w1_raw = {}
+        w1_w = {(1, a): held([P, KP], U32, "w1_w1%d" % a) for a in range(2)}
         w1_s = {(b, a): held([P, KP], U8, "w1_s%d%d" % (b, a)) for b in range(2) for a in range(2)}
-        w3_raw = held([P, PACK, N], F32, "w3_raw")
         w3_w = held([P, N], U32, "w3_w")
         w3_s = held([P, N], U8, "w3_s")
-        w2_raw_w = held([P, 2, 2 * N], U8, "w2_raw_w")
-        w2_raw_s = held([P, 2, N], U8, "w2_raw_s")
+        w2_raw_w = placed([P, 2, 2 * N], U8, "w2_raw_w", TAB1)
         w2_w = held([P, 2, 2 * N], U8, "w2_w")
-        w2_s = held([P, 2, N], U8, "w2_s")
         b1_sb = held([P, 2, PACK], F32, "b1_sb")
         gh_sb = held([P, 2, PACK], F32, "gh_sb")
         gb_sb = held([P, 2, PACK], F32, "gb_sb")
@@ -70,71 +70,84 @@ def tile_list_session_tolerance_bound_kernel(
         y_s = held([P, R], U8, "y_s")
 
         nc.vector.memset(tab_s[:].bitcast(I32), 0)
-        nc.vector.memset(tab2_s[:].bitcast(I32), 0)
-        nc.vector.memset(w2_raw_s[:].rearrange("p a n -> p (a n)").bitcast(I32), 0)
 
         def words(ap):
             return ap.rearrange("p n t -> p (n t)").bitcast(I32)
 
         def load_w1(b, a):
+            w1_raw[b, a] = ring.tile([P, PACK, KP], F32, name="w1_raw", tag="raw", align_bytes=64)
             rows = w1[a * KP : (a + 1) * KP, b * KP : (b + 1) * KP]
             nc.sync.dma_start(out=w1_raw[b, a][:], in_=rows.rearrange("(p i) c -> p i c", i=PACK))
 
         nc.sync.dma_start(offs_sb[:], offs)
         nc.sync.dma_start(offs2_sb[:], offs2)
+        nc.sync.dma_start(pos1_sb[:], pos1)
+        nc.gpsimd.dma_start(out=b1_sb[:], in_=b1.rearrange("(b p t) -> p b t", b=2, t=PACK))
+        nc.gpsimd.dma_start(out=gh_sb[:], in_=gh.rearrange("(b p t) -> p b t", b=2, t=PACK))
+        nc.gpsimd.dma_start(out=tol_sb[:], in_=tol.rearrange("(p t) -> p t", t=PACK))
+        nc.sync.dma_start(out=w2_raw_w[:].bitcast(I32), in_=w2_words.rearrange("a p n -> p a n").bitcast(I32))
         nc.sync.dma_start(out=tab_w[0][:].bitcast(I32), in_=words(tab_words[0]))
-        for q in range(4):
-            nc.gpsimd.dma_start(
-                out=tab_s[32 * q : 32 * q + 8, :].bitcast(I32), in_=tab_scales[:, 4 * q : 4 * q + 4, :].bitcast(I32)
-            )
-        for q in range(4):
-            nc.gpsimd.dma_start(
-                out=tab2_s[32 * q : 32 * q + 4, :].bitcast(I32), in_=tab2_scales[0, 4 * q : 4 * q + 4, :].bitcast(I32)
-            )
-        for q in range(4):
-            nc.gpsimd.dma_start(
-                out=w2_raw_s[32 * q : 32 * q + 4, :, :].bitcast(I32),
-                in_=w2_scales[:, 4 * q : 4 * q + 4, :].rearrange("a r n -> r a n").bitcast(I32),
-            )
         load_w1(0, 0)
         load_w1(0, 1)
-        nc.sync.dma_start(out=w2_raw_w[:].bitcast(I32), in_=w2_words.rearrange("a p n -> p a n").bitcast(I32))
-        nc.sync.dma_start(out=b1_sb[:], in_=b1.rearrange("(b p t) -> p b t", b=2, t=PACK))
-        nc.sync.dma_start(out=gh_sb[:], in_=gh.rearrange("(b p t) -> p b t", b=2, t=PACK))
-        nc.sync.dma_start(out=tab_w[1][:].bitcast(I32), in_=words(tab_words[1]))
-        load_w1(1, 0)
-        load_w1(1, 1)
-        nc.sync.dma_start(out=tab2_w[:].bitcast(I32), in_=words(tab2_words[0]))
-        nc.sync.dma_start(out=w3_raw[:], in_=w3.rearrange("(p i) c -> p i c", i=PACK))
-        nc.sync.dma_start(pos1_sb[:], pos1)
-        nc.sync.dma_start(out=tol_sb[:], in_=tol.rearrange("(p t) -> p t", t=PACK))
+        for q in range(4):
+            nc.sync.dma_start(
+                out=tab_s[32 * q : 32 * q + 8, :].bitcast(I32), in_=tab_scales[:, 4 * q : 4 * q + 4, :].bitcast(I32)
+            )
 
-        def deal(raw, grouped):
+        def deal(raw, grouped, scalar_m):
             src = raw[:].rearrange("p i (m t) -> p m i t", t=PACK)
             dst = grouped[:].rearrange("p (t m i) -> p m i t", t=PACK, i=PACK)
-            for m0 in range(0, P, 32):
+            for m0 in range(0, scalar_m, 32):
                 nc.scalar.copy(out=dst[:, m0 : m0 + 32], in_=src[:, m0 : m0 + 32])
+            if scalar_m < P:
+                nc.vector.tensor_copy(out=dst[:, scalar_m:], in_=src[:, scalar_m:])
 
         def quantize(codes, scales, grouped):
             nc.vector.quantize_mx(out=codes.bitcast(FP8X4), scales=scales, in_=grouped)
 
-        nc.vector.tensor_copy(out=v_s[:], in_=tab_s[:].indirect(offs_sb[:]))
-        nc.vector.tensor_copy(out=v_w[0][:], in_=tab_w[0][:].indirect(offs_sb[:]))
-        nc.vector.tensor_copy(out=v2_s[:], in_=tab2_s[:].indirect(offs2_sb[:]))
-        for a in range(2):
-            deal(w1_raw[0, a], w1_bf[0, a])
-            quantize(w1_w[0, a][:], w1_s[0, a][:], w1_bf[0, a][:])
+        nc.gpsimd.tensor_tensor(out=gb_sb[:], in0=gh_sb[:], in1=b1_sb[:], op=ALU.mult)
         nc.vector.tensor_copy(
             out=w2_w[:].bitcast(U16).rearrange("p a (t m) -> p a m t", t=PACK),
             in_=w2_raw_w[:].bitcast(U16).rearrange("p a (m t) -> p a m t", t=PACK),
         )
-        nc.vector.tensor_tensor(out=gb_sb[:], in0=gh_sb[:], in1=b1_sb[:], op=ALU.mult)
+        tab_w[1] = placed([P, T], U32, "tab_w1", TAB1)
+        nc.sync.dma_start(out=tab_w[1][:].bitcast(I32), in_=words(tab_words[1]))
+        nc.vector.tensor_copy(out=v_w[0][:], in_=tab_w[0][:].indirect(offs_sb[:]))
+        w1_bf = placed([P, PACK * KP], BF16, "w1_bf00", 0)
+        deal(w1_raw[0, 0], w1_bf, P)
+        v_s = placed([P, S], U8, "v_s", 8192)
+        nc.vector.tensor_copy(out=v_s[:], in_=tab_s[:].indirect(offs_sb[:]))
+        for a in range(2):
+            w1_w[0, a] = placed([P, KP], U32, "w1_w0%d" % a, SCALES + 2048 * a)
+        quantize(w1_w[0, 0][:], w1_s[0, 0][:], w1_bf[:])
+        w1_bf = placed([P, PACK * KP], BF16, "w1_bf01", 4096)
+        deal(w1_raw[0, 1], w1_bf, P)
+        quantize(w1_w[0, 1][:], w1_s[0, 1][:], w1_bf[:])
+        load_w1(1, 0)
+        load_w1(1, 1)
+        w2_raw_s = placed([P, 2, N], U8, "w2_raw_s", 0)
+        tab2_s = placed([P, T2], U8, "tab2_s", 1024)
+        nc.gpsimd.memset(w2_raw_s[:].rearrange("p a n -> p (a n)").bitcast(I32), 0)
+        nc.gpsimd.memset(tab2_s[:].bitcast(I32), 0)
+        for q in range(4):
+            nc.sync.dma_start(
+                out=w2_raw_s[32 * q : 32 * q + 4, :, :].bitcast(I32),
+                in_=w2_scales[:, 4 * q : 4 * q + 4, :].rearrange("a r n -> r a n").bitcast(I32),
+            )
+        for q in range(4):
+            nc.sync.dma_start(
+                out=tab2_s[32 * q : 32 * q + 4, :].bitcast(I32), in_=tab2_scales[0, 4 * q : 4 * q + 4, :].bitcast(I32)
+            )
         for half in range(2):
             nc.vector.tensor_copy(
                 out=v_w[1][:, 512 * half : 512 * (half + 1)], in_=tab_w[1][:].indirect(offs_sb[:, 32 * half : 32 * (half + 1)])
             )
 
-        def first_stage(b, j0, n, road):
+        tab2_w = placed([P, T2], U32, "tab2_w", TAB1)
+        nc.sync.dma_start(out=tab2_w[:].bitcast(I32), in_=words(tab2_words[0]))
+
+        def first_stage(g):
+            b, j0, n, road = H_GROUPS[g]
             cols = slice(j0, j0 + n)
             if road == "x":
                 planes = ring.tile([P, PACK, n], F32, name="planes", tag="planes", align_bytes=64)
@@ -153,7 +166,8 @@ def tile_list_session_tolerance_bound_kernel(
                         start=(a == 0),
                         stop=(a == 1),
                     )
-                sine = sring.tile([P, n], F32, name="sine", tag="sine")
+                slot = PACK * (g % 2) + t
+                sine = placed([P, n], F32, "sine%d" % slot, SINES + 2048 * slot)
                 nc.scalar.activation(out=sine[:], in_=acc[:], func=ACT.Sin, bias=b1_sb[:, b, t : t + 1])
                 if road == "x":
                     nc.vector.scalar_tensor_tensor(
@@ -167,6 +181,10 @@ def tile_list_session_tolerance_bound_kernel(
                     nc.vector.scalar_tensor_tensor(
                         out=planes[:, t, :], in0=sine[:], scalar=gh_sb[:, b, t : t + 1], in1=gained[:], op0=ALU.mult, op1=ALU.add
                     )
+            return planes
+
+        def finish_h(g, planes):
+            b, j0, n, road = H_GROUPS[g]
             grouped = ring.tile([P, n * PACK], BF16, name="h_bf", tag="h_bf", align_bytes=64)
             src = planes[:].rearrange("p t (c i) -> p c t i", i=RUN)
             dst = grouped[:].rearrange("p (c i t) -> p c t i", i=RUN, t=PACK)
@@ -175,9 +193,10 @@ def tile_list_session_tolerance_bound_kernel(
                 nc.vector.tensor_tensor(out=dst, in0=src, in1=gain, op=ALU.mult)
             else:
                 nc.vector.tensor_copy(out=dst, in_=src)
-            return grouped
+            quantize(h_w[b][:, j0 : j0 + n], h_s[b][:, j0 : j0 + n], grouped[:])
 
-        def second_stage(j0, n):
+        def second_stage(g):
+            b, j0, n, road = H_GROUPS[g]
             cols = slice(j0, j0 + n)
             for t in range(PACK):
                 dacc = psum.tile([P, n], F32, name="dacc", tag="dacc")
@@ -193,35 +212,44 @@ def tile_list_session_tolerance_bound_kernel(
                     )
                 nc.scalar.copy(out=d_sb[t][:, cols], in_=dacc[:])
 
-        for g, (b, j0, n, road) in enumerate(H_GROUPS):
-            grouped = first_stage(b, j0, n, road)
-            quantize(h_w[b][:, j0 : j0 + n], h_s[b][:, j0 : j0 + n], grouped[:])
-            if g == 1:
-                deal(w1_raw[1, 0], w1_bf[1, 0])
-                quantize(w1_w[1, 0][:], w1_s[1, 0][:], w1_bf[1, 0][:])
-                deal(w1_raw[1, 1], w1_bf[1, 1])
-                quantize(w1_w[1, 1][:], w1_s[1, 1][:], w1_bf[1, 1][:])
-                nc.vector.tensor_copy(
-                    out=w2_s[:].rearrange("p a (t m) -> p a m t", t=PACK),
-                    in_=w2_raw_s[:].rearrange("p a (m t) -> p a m t", t=PACK),
-                )
-            if g > 0 and H_GROUPS[g - 1][0] == 1:
-                second_stage(*H_GROUPS[g - 1][1:3])
-        second_stage(*H_GROUPS[-1][1:3])
+        planes = first_stage(0)
+        w1_bf = placed([P, PACK * KP], BF16, "w1_bf10", SINES)
+        deal(w1_raw[1, 0], w1_bf, P)
+        w3_raw = ring.tile([P, PACK, N], F32, name="w3_raw", tag="raw", align_bytes=64)
+        nc.sync.dma_start(out=w3_raw[:], in_=w3.rearrange("(p i) c -> p i c", i=PACK))
+        finish_h(0, planes)
+        quantize(w1_w[1, 0][:], w1_s[1, 0][:], w1_bf[:])
+        planes = first_stage(1)
+        w1_bf = placed([P, PACK * KP], BF16, "w1_bf11", SINES + 4096)
+        deal(w1_raw[1, 1], w1_bf, 96)
+        quantize(w1_w[1, 1][:], w1_s[1, 1][:], w1_bf[:])
+        finish_h(1, planes)
+        w2_s = placed([P, 2, N], U8, "w2_s", SCALES)
+        nc.vector.tensor_copy(
+            out=w2_s[:].rearrange("p a (t m) -> p a m t", t=PACK),
+            in_=w2_raw_s[:].rearrange("p a (m t) -> p a m t", t=PACK),
+        )
+        for g in range(2, len(H_GROUPS)):
+            finish_h(g, first_stage(g))
+        for g in range(2, len(H_GROUPS)):
+            second_stage(g)
 
-        w3_bf = ring.tile([P, PACK * N], BF16, name="w3_bf", tag="h_bf", align_bytes=64)
-        deal(w3_raw, w3_bf)
+        w3_bf = placed([P, PACK * N], BF16, "w3_bf", SINES)
+        deal(w3_raw, w3_bf, P)
         v2_w = ring.tile([P, R], U32, name="v2_w", tag="h_bf", align_bytes=64)
+        v2_s = ring.tile([P, R], U8, name="v2_s", tag="planes", align_bytes=64)
+        nc.vector.tensor_copy(out=v2_s[:], in_=tab2_s[:].indirect(offs2_sb[:]))
         nc.vector.tensor_copy(out=v2_w[:], in_=tab2_w[:].indirect(offs2_sb[:]))
 
         picked = {}
 
-        def pick(j0, n):
-            for t in range(PACK):
-                picked[j0, t] = held([P, n], F32, "picked%d_%d" % (j0, t))
-                nc.vector.tensor_copy(out=picked[j0, t][:], in_=d_sb[t][:].indirect(pos1_sb[:, j0 // 16 : (j0 + n) // 16]))
+        def pick(t):
+            picked[t] = placed([P, R], F32, "picked%d" % t, SINES + 2048 * (PACK + 1 - t) if t < 3 else SINES)
+            nc.vector.tensor_copy(out=picked[t][:], in_=d_sb[t][:].indirect(pos1_sb[:]))
 
-        pick(*Y_CHUNKS[0])
+        pick(0)
+        pick(1)
+        pick(2)
         quantize(w3_w[:], w3_s[:], w3_bf[:])
         b_acc = []
         for t in range(PACK):
@@ -237,7 +265,7 @@ def tile_list_session_tolerance_bound_kernel(
                 stop=True,
             )
             b_acc.append(acc)
-        pick(*Y_CHUNKS[1])
+        pick(3)
 
         out_rows = out_0.rearrange("(p t) j -> p t j", t=PACK)
         out_words = words(out_1[0])
@@ -248,7 +276,7 @@ def tile_list_session_tolerance_bound_kernel(
             y[j0] = held([P, PACK, n], F32, "y%d" % j0)
             for t in range(PACK):
                 lower = sring.tile([P, n], F32, name="lower", tag="gained")
-                nc.vector.tensor_tensor(out=lower[:], in0=picked[j0, t][:], in1=b_acc[t][:, cols], op=ALU.min)
+                nc.vector.tensor_tensor(out=lower[:], in0=picked[t][:, cols], in1=b_acc[t][:, cols], op=ALU.min)
                 nc.scalar.activation(out=y[j0][:, t, :], in_=lower[:], func=ACT.Copy, scale=tol_sb[:, t : t + 1])
             nc.sync.dma_start(out=out_rows[:, :, cols], in_=y[j0][:])
             y_bf[j0] = held([P, n * PACK], BF16, "y_bf%d" % j0)
@@ -257,9 +285,9 @@ def tile_list_session_tolerance_bound_kernel(
             src = y[j0][:].rearrange("p t (c i) -> p c t i", i=RUN)
             dst = y_bf[j0][:].rearrange("p (c i t) -> p c t i", i=RUN, t=PACK)
             if j0 == 0:
-                nc.scalar.copy(out=dst, in_=src)
-            else:
                 nc.vector.tensor_copy(out=dst, in_=src)
+            else:
+                nc.scalar.copy(out=dst, in_=src)
             quantize(y_w[:, cols], y_s[:, cols], y_bf[j0][:])
             nc.sync.dma_start(out=out_words[:, cols], in_=y_w[:, cols].bitcast(I32))
         for q in range(4):

@@ -19,7 +19,7 @@ ALU = mybir.AluOpType
 P = 128
 PACK = 4
 KP = P * PACK
-RUN = 4
+RUN = 2
 SINES = 16384
 TAB1 = 32768
 SCALES = 49152
@@ -69,7 +69,11 @@ def tile_list_session_tolerance_bound_kernel(
         y_w = held([P, R], U32, "y_w")
         y_s = held([P, R], U8, "y_s")
 
+        tab2_s = placed([P, T2], U8, "tab2_s", SCALES + 4096)
+        w2_raw_s = held([P, 2, N], U8, "w2_raw_s")
         nc.vector.memset(tab_s[:].bitcast(I32), 0)
+        nc.vector.memset(tab2_s[:].bitcast(I32), 0)
+        nc.vector.memset(w2_raw_s[:].rearrange("p a n -> p (a n)").bitcast(I32), 0)
 
         def words(ap):
             return ap.rearrange("p n t -> p (n t)").bitcast(I32)
@@ -80,18 +84,27 @@ def tile_list_session_tolerance_bound_kernel(
             nc.sync.dma_start(out=w1_raw[b, a][:], in_=rows.rearrange("(p i) c -> p i c", i=PACK))
 
         nc.sync.dma_start(offs_sb[:], offs)
-        nc.sync.dma_start(offs2_sb[:], offs2)
-        nc.sync.dma_start(pos1_sb[:], pos1)
-        nc.gpsimd.dma_start(out=b1_sb[:], in_=b1.rearrange("(b p t) -> p b t", b=2, t=PACK))
-        nc.gpsimd.dma_start(out=gh_sb[:], in_=gh.rearrange("(b p t) -> p b t", b=2, t=PACK))
-        nc.gpsimd.dma_start(out=tol_sb[:], in_=tol.rearrange("(p t) -> p t", t=PACK))
+        nc.scalar.dma_start(out=b1_sb[:], in_=b1.rearrange("(b p t) -> p b t", b=2, t=PACK))
+        nc.scalar.dma_start(out=gh_sb[:], in_=gh.rearrange("(b p t) -> p b t", b=2, t=PACK))
+        nc.scalar.dma_start(out=tol_sb[:], in_=tol.rearrange("(p t) -> p t", t=PACK))
         nc.sync.dma_start(out=w2_raw_w[:].bitcast(I32), in_=w2_words.rearrange("a p n -> p a n").bitcast(I32))
         nc.sync.dma_start(out=tab_w[0][:].bitcast(I32), in_=words(tab_words[0]))
         load_w1(0, 0)
         load_w1(0, 1)
+        nc.sync.dma_start(offs2_sb[:], offs2)
+        nc.sync.dma_start(pos1_sb[:], pos1)
         for q in range(4):
-            nc.sync.dma_start(
+            nc.gpsimd.dma_start(
                 out=tab_s[32 * q : 32 * q + 8, :].bitcast(I32), in_=tab_scales[:, 4 * q : 4 * q + 4, :].bitcast(I32)
+            )
+        for q in range(4):
+            nc.gpsimd.dma_start(
+                out=tab2_s[32 * q : 32 * q + 4, :].bitcast(I32), in_=tab2_scales[0, 4 * q : 4 * q + 4, :].bitcast(I32)
+            )
+        for q in range(4):
+            nc.gpsimd.dma_start(
+                out=w2_raw_s[32 * q : 32 * q + 4, :, :].bitcast(I32),
+                in_=w2_scales[:, 4 * q : 4 * q + 4, :].rearrange("a r n -> r a n").bitcast(I32),
             )
 
         def deal(raw, grouped, scalar_m):
@@ -105,7 +118,7 @@ def tile_list_session_tolerance_bound_kernel(
         def quantize(codes, scales, grouped):
             nc.vector.quantize_mx(out=codes.bitcast(FP8X4), scales=scales, in_=grouped)
 
-        nc.gpsimd.tensor_tensor(out=gb_sb[:], in0=gh_sb[:], in1=b1_sb[:], op=ALU.mult)
+        nc.vector.tensor_tensor(out=gb_sb[:], in0=gh_sb[:], in1=b1_sb[:], op=ALU.mult)
         nc.vector.tensor_copy(
             out=w2_w[:].bitcast(U16).rearrange("p a (t m) -> p a m t", t=PACK),
             in_=w2_raw_w[:].bitcast(U16).rearrange("p a (m t) -> p a m t", t=PACK),
@@ -117,32 +130,26 @@ def tile_list_session_tolerance_bound_kernel(
         deal(w1_raw[0, 0], w1_bf, P)
         v_s = placed([P, S], U8, "v_s", 8192)
         nc.vector.tensor_copy(out=v_s[:], in_=tab_s[:].indirect(offs_sb[:]))
-        for a in range(2):
-            w1_w[0, a] = placed([P, KP], U32, "w1_w0%d" % a, SCALES + 2048 * a)
+        w1_w[0, 0] = placed([P, KP], U32, "w1_w00", SCALES)
         quantize(w1_w[0, 0][:], w1_s[0, 0][:], w1_bf[:])
+        v2_s = placed([P, R], U8, "v2_s", 0)
+        nc.vector.tensor_copy(out=v2_s[:], in_=tab2_s[:].indirect(offs2_sb[:]))
+        w1_w[0, 1] = placed([P, KP], U32, "w1_w01", SCALES + 4096)
         w1_bf = placed([P, PACK * KP], BF16, "w1_bf01", 4096)
         deal(w1_raw[0, 1], w1_bf, P)
         quantize(w1_w[0, 1][:], w1_s[0, 1][:], w1_bf[:])
         load_w1(1, 0)
         load_w1(1, 1)
-        w2_raw_s = placed([P, 2, N], U8, "w2_raw_s", 0)
-        tab2_s = placed([P, T2], U8, "tab2_s", 1024)
-        nc.gpsimd.memset(w2_raw_s[:].rearrange("p a n -> p (a n)").bitcast(I32), 0)
-        nc.gpsimd.memset(tab2_s[:].bitcast(I32), 0)
-        for q in range(4):
-            nc.sync.dma_start(
-                out=w2_raw_s[32 * q : 32 * q + 4, :, :].bitcast(I32),
-                in_=w2_scales[:, 4 * q : 4 * q + 4, :].rearrange("a r n -> r a n").bitcast(I32),
-            )
-        for q in range(4):
-            nc.sync.dma_start(
-                out=tab2_s[32 * q : 32 * q + 4, :].bitcast(I32), in_=tab2_scales[0, 4 * q : 4 * q + 4, :].bitcast(I32)
-            )
         for half in range(2):
             nc.vector.tensor_copy(
                 out=v_w[1][:, 512 * half : 512 * (half + 1)], in_=tab_w[1][:].indirect(offs_sb[:, 32 * half : 32 * (half + 1)])
             )
 
+        w2_s = placed([P, 2, N], U8, "w2_s", TAB1 + 8192)
+        nc.vector.tensor_copy(
+            out=w2_s[:].rearrange("p a (t m) -> p a m t", t=PACK),
+            in_=w2_raw_s[:].rearrange("p a (m t) -> p a m t", t=PACK),
+        )
         tab2_w = placed([P, T2], U32, "tab2_w", TAB1)
         nc.sync.dma_start(out=tab2_w[:].bitcast(I32), in_=words(tab2_words[0]))
 
@@ -186,10 +193,11 @@ def tile_list_session_tolerance_bound_kernel(
         def finish_h(g, planes):
             b, j0, n, road = H_GROUPS[g]
             grouped = ring.tile([P, n * PACK], BF16, name="h_bf", tag="h_bf", align_bytes=64)
-            src = planes[:].rearrange("p t (c i) -> p c t i", i=RUN)
-            dst = grouped[:].rearrange("p (c i t) -> p c t i", i=RUN, t=PACK)
+            run = 2 if road == "x" else 4
+            src = planes[:].rearrange("p t (c i) -> p c t i", i=run)
+            dst = grouped[:].rearrange("p (c i t) -> p c t i", i=run, t=PACK)
             if road == "x":
-                gain = gh_sb[:, b, :].unsqueeze(1).unsqueeze(3).broadcast_to([P, n // RUN, PACK, RUN])
+                gain = gh_sb[:, b, :].unsqueeze(1).unsqueeze(3).broadcast_to([P, n // run, PACK, run])
                 nc.vector.tensor_tensor(out=dst, in0=src, in1=gain, op=ALU.mult)
             else:
                 nc.vector.tensor_copy(out=dst, in_=src)
@@ -224,11 +232,6 @@ def tile_list_session_tolerance_bound_kernel(
         deal(w1_raw[1, 1], w1_bf, 96)
         quantize(w1_w[1, 1][:], w1_s[1, 1][:], w1_bf[:])
         finish_h(1, planes)
-        w2_s = placed([P, 2, N], U8, "w2_s", SCALES)
-        nc.vector.tensor_copy(
-            out=w2_s[:].rearrange("p a (t m) -> p a m t", t=PACK),
-            in_=w2_raw_s[:].rearrange("p a (m t) -> p a m t", t=PACK),
-        )
         for g in range(2, len(H_GROUPS)):
             finish_h(g, first_stage(g))
         for g in range(2, len(H_GROUPS)):
@@ -237,8 +240,6 @@ def tile_list_session_tolerance_bound_kernel(
         w3_bf = placed([P, PACK * N], BF16, "w3_bf", SINES)
         deal(w3_raw, w3_bf, P)
         v2_w = ring.tile([P, R], U32, name="v2_w", tag="h_bf", align_bytes=64)
-        v2_s = ring.tile([P, R], U8, name="v2_s", tag="planes", align_bytes=64)
-        nc.vector.tensor_copy(out=v2_s[:], in_=tab2_s[:].indirect(offs2_sb[:]))
         nc.vector.tensor_copy(out=v2_w[:], in_=tab2_w[:].indirect(offs2_sb[:]))
 
         picked = {}

@@ -21,9 +21,11 @@ PACK = 4
 KP = P * PACK
 RUN = 2
 SINES = 16384
-TAB1 = 32768
-SCALES = 49152
-H_GROUPS = [(0, 0, 512, "x"), (0, 512, 512, "x"), (1, 0, 512, "x"), (1, 512, 256, "a"), (1, 768, 256, "a")]
+TAB1 = 37888
+SCALES = 55296
+LAST = 11264
+EXTRA = 61440
+H_GROUPS = [(0, 0, 512, "x"), (0, 512, 512, "x"), (1, 0, 512, "x"), (1, 512, 512, "a")]
 Y_CHUNKS = [(0, 384), (384, 128)]
 
 
@@ -53,9 +55,8 @@ def tile_list_session_tolerance_bound_kernel(
         tab_s = placed([P, T], U8, "tab_s", SCALES)
         v_w = [held([P, S], U32, "v_w%d" % a) for a in range(2)]
         w1_raw = {}
-        w1_w = {(1, a): held([P, KP], U32, "w1_w1%d" % a) for a in range(2)}
+        w1_w = {(1, 1): held([P, KP], U32, "w1_w11")}
         w1_s = {(b, a): held([P, KP], U8, "w1_s%d%d" % (b, a)) for b in range(2) for a in range(2)}
-        w3_w = held([P, N], U32, "w3_w")
         w3_s = held([P, N], U8, "w3_s")
         w2_raw_w = placed([P, 2, 2 * N], U8, "w2_raw_w", TAB1)
         w2_w = held([P, 2, 2 * N], U8, "w2_w")
@@ -145,12 +146,14 @@ def tile_list_session_tolerance_bound_kernel(
                 out=v_w[1][:, 512 * half : 512 * (half + 1)], in_=tab_w[1][:].indirect(offs_sb[:, 32 * half : 32 * (half + 1)])
             )
 
-        w2_s = placed([P, 2, N], U8, "w2_s", TAB1 + 8192)
+        w2_s = placed([P, 2, N], U8, "w2_s", TAB1 - 512)
         nc.vector.tensor_copy(
             out=w2_s[:].rearrange("p a (t m) -> p a m t", t=PACK),
             in_=w2_raw_s[:].rearrange("p a (m t) -> p a m t", t=PACK),
         )
-        tab2_w = placed([P, T2], U32, "tab2_w", TAB1)
+        w3_raw = placed([P, PACK, N], F32, "w3_raw", TAB1 + 8704)
+        nc.sync.dma_start(out=w3_raw[:], in_=w3.rearrange("(p i) c -> p i c", i=PACK))
+        tab2_w = placed([P, T2], U32, "tab2_w", TAB1 + 512)
         nc.sync.dma_start(out=tab2_w[:].bitcast(I32), in_=words(tab2_words[0]))
 
         def first_stage(g):
@@ -173,8 +176,11 @@ def tile_list_session_tolerance_bound_kernel(
                         start=(a == 0),
                         stop=(a == 1),
                     )
-                slot = PACK * (g % 2) + t
-                sine = placed([P, n], F32, "sine%d" % slot, SINES + 2048 * slot)
+                if g == 2:
+                    sine = placed([P, n], F32, "sine_third%d" % t, EXTRA + 2048 * t)
+                else:
+                    slot = PACK * (g == 1) + t
+                    sine = placed([P, n], F32, "sine%d" % slot, SINES + 2048 * slot)
                 nc.scalar.activation(out=sine[:], in_=acc[:], func=ACT.Sin, bias=b1_sb[:, b, t : t + 1])
                 if road == "x":
                     nc.vector.scalar_tensor_tensor(
@@ -192,7 +198,12 @@ def tile_list_session_tolerance_bound_kernel(
 
         def finish_h(g, planes):
             b, j0, n, road = H_GROUPS[g]
-            grouped = ring.tile([P, n * PACK], BF16, name="h_bf", tag="h_bf", align_bytes=64)
+            if g == len(H_GROUPS) - 1:
+                grouped = placed([P, n * PACK], BF16, "h_bf_last", LAST)
+            elif g == 1:
+                grouped = placed([P, n * PACK], BF16, "h_bf_second", SINES + 4096)
+            else:
+                grouped = ring.tile([P, n * PACK], BF16, name="h_bf", tag="h_bf", align_bytes=64)
             run = 2 if road == "x" else 4
             src = planes[:].rearrange("p t (c i) -> p c t i", i=run)
             dst = grouped[:].rearrange("p (c i t) -> p c t i", i=run, t=PACK)
@@ -203,54 +214,48 @@ def tile_list_session_tolerance_bound_kernel(
                 nc.vector.tensor_copy(out=dst, in_=src)
             quantize(h_w[b][:, j0 : j0 + n], h_s[b][:, j0 : j0 + n], grouped[:])
 
-        def second_stage(g):
-            b, j0, n, road = H_GROUPS[g]
-            cols = slice(j0, j0 + n)
+        def second_stage(groups):
+            first = H_GROUPS[groups[0]][1]
             for t in range(PACK):
-                dacc = psum.tile([P, n], F32, name="dacc", tag="dacc")
-                for b in range(2):
-                    nc.tensor.matmul_mx(
-                        out=dacc[:],
-                        lhsT=w2_w[:, b, 2 * P * t : 2 * P * (t + 1)].bitcast(FP4X4),
-                        lhsT_scale=w2_s[:, b, P * t : P * (t + 1)],
-                        rhs=h_w[b][:, cols].bitcast(FP8X4),
-                        rhs_scale=h_s[b][:, cols],
-                        start=(b == 0),
-                        stop=(b == 1),
-                    )
-                nc.scalar.copy(out=d_sb[t][:, cols], in_=dacc[:])
+                dacc = psum.tile([P, KP], F32, name="dacc", tag="dacc")
+                for g in groups:
+                    j0, n = H_GROUPS[g][1:3]
+                    cols = slice(j0, j0 + n)
+                    for b in range(2):
+                        nc.tensor.matmul_mx(
+                            out=dacc[:, j0 - first : j0 - first + n],
+                            lhsT=w2_w[:, b, 2 * P * t : 2 * P * (t + 1)].bitcast(FP4X4),
+                            lhsT_scale=w2_s[:, b, P * t : P * (t + 1)],
+                            rhs=h_w[b][:, cols].bitcast(FP8X4),
+                            rhs_scale=h_s[b][:, cols],
+                            start=(b == 0),
+                            stop=(b == 1),
+                        )
+                nc.scalar.copy(out=d_sb[t][:, first : first + KP], in_=dacc[:])
 
         planes = first_stage(0)
-        w1_bf = placed([P, PACK * KP], BF16, "w1_bf10", SINES)
-        deal(w1_raw[1, 0], w1_bf, P)
-        w3_raw = ring.tile([P, PACK, N], F32, name="w3_raw", tag="raw", align_bytes=64)
-        nc.sync.dma_start(out=w3_raw[:], in_=w3.rearrange("(p i) c -> p i c", i=PACK))
         finish_h(0, planes)
-        quantize(w1_w[1, 0][:], w1_s[1, 0][:], w1_bf[:])
         planes = first_stage(1)
-        w1_bf = placed([P, PACK * KP], BF16, "w1_bf11", SINES + 4096)
-        deal(w1_raw[1, 1], w1_bf, 96)
-        quantize(w1_w[1, 1][:], w1_s[1, 1][:], w1_bf[:])
+        w1_bf10 = placed([P, PACK * KP], BF16, "w1_bf10", SINES)
+        deal(w1_raw[1, 0], w1_bf10, P)
+        w1_bf11 = placed([P, PACK * KP], BF16, "w1_bf11", SINES + 4096)
+        deal(w1_raw[1, 1], w1_bf11, 64)
+        w1_w[1, 0] = placed([P, KP], U32, "w1_w10", SINES + 2048 * 7)
+        quantize(w1_w[1, 0][:], w1_s[1, 0][:], w1_bf10[:])
+        quantize(w1_w[1, 1][:], w1_s[1, 1][:], w1_bf11[:])
         finish_h(1, planes)
-        for g in range(2, len(H_GROUPS)):
-            finish_h(g, first_stage(g))
-        for g in range(2, len(H_GROUPS)):
-            second_stage(g)
-
-        w3_bf = placed([P, PACK * N], BF16, "w3_bf", SINES)
+        planes = first_stage(2)
+        w3_bf = placed([P, PACK * N], BF16, "w3_bf", SINES + 8192)
         deal(w3_raw, w3_bf, P)
-        v2_w = ring.tile([P, R], U32, name="v2_w", tag="h_bf", align_bytes=64)
+        finish_h(2, planes)
+        for g in range(3, len(H_GROUPS)):
+            finish_h(g, first_stage(g))
+        second_stage([2])
+        second_stage([3])
+
+        v2_w = placed([P, R], U32, "v2_w", LAST - 1024)
         nc.vector.tensor_copy(out=v2_w[:], in_=tab2_w[:].indirect(offs2_sb[:]))
-
-        picked = {}
-
-        def pick(t):
-            picked[t] = placed([P, R], F32, "picked%d" % t, SINES + 2048 * (PACK + 1 - t) if t < 3 else SINES)
-            nc.vector.tensor_copy(out=picked[t][:], in_=d_sb[t][:].indirect(pos1_sb[:]))
-
-        pick(0)
-        pick(1)
-        pick(2)
+        w3_w = placed([P, N], U32, "w3_w", LAST + 1024)
         quantize(w3_w[:], w3_s[:], w3_bf[:])
         b_acc = []
         for t in range(PACK):
@@ -266,30 +271,41 @@ def tile_list_session_tolerance_bound_kernel(
                 stop=True,
             )
             b_acc.append(acc)
-        pick(3)
 
         out_rows = out_0.rearrange("(p t) j -> p t j", t=PACK)
         out_words = words(out_1[0])
-        y_bf = {}
-        y = {}
+        y = held([P, PACK, R], F32, "y")
+        y_bf = held([P, PACK * R], BF16, "y_bf")
+
+        def pick(t, j0, n):
+            picked = ring.tile([P, n], F32, name="picked", tag="picked")
+            nc.vector.tensor_copy(out=picked[:], in_=d_sb[t][:].indirect(pos1_sb[:, j0 // 16 : (j0 + n) // 16]))
+            return picked
+
+        def bound(t, j0, n, picked):
+            cols = slice(j0, j0 + n)
+            lower = sring.tile([P, n], F32, name="lower", tag="gained")
+            nc.vector.tensor_tensor(out=lower[:], in0=picked[:], in1=b_acc[t][:, cols], op=ALU.min)
+            nc.scalar.activation(out=y[:, t, cols], in_=lower[:], func=ACT.Copy, scale=tol_sb[:, t : t + 1])
+            nc.sync.dma_start(out=out_rows[:, t, cols], in_=y[:, t, cols])
+
+        pieces = [(t, 0, R) for t in range(PACK - 1)] + [(PACK - 1, j0, n) for j0, n in Y_CHUNKS]
+        ahead = pick(*pieces[0])
+        for piece, following in zip(pieces, pieces[1:] + [None]):
+            picked = ahead
+            if following is not None:
+                ahead = pick(*following)
+            bound(*piece, picked)
         for j0, n in Y_CHUNKS:
             cols = slice(j0, j0 + n)
-            y[j0] = held([P, PACK, n], F32, "y%d" % j0)
-            for t in range(PACK):
-                lower = sring.tile([P, n], F32, name="lower", tag="gained")
-                nc.vector.tensor_tensor(out=lower[:], in0=picked[t][:, cols], in1=b_acc[t][:, cols], op=ALU.min)
-                nc.scalar.activation(out=y[j0][:, t, :], in_=lower[:], func=ACT.Copy, scale=tol_sb[:, t : t + 1])
-            nc.sync.dma_start(out=out_rows[:, :, cols], in_=y[j0][:])
-            y_bf[j0] = held([P, n * PACK], BF16, "y_bf%d" % j0)
-        for j0, n in Y_CHUNKS:
-            cols = slice(j0, j0 + n)
-            src = y[j0][:].rearrange("p t (c i) -> p c t i", i=RUN)
-            dst = y_bf[j0][:].rearrange("p (c i t) -> p c t i", i=RUN, t=PACK)
+            grouped = y_bf[:, PACK * j0 : PACK * (j0 + n)]
+            src = y[:, :, cols].rearrange("p t (c i) -> p c t i", i=RUN)
+            dst = grouped.rearrange("p (c i t) -> p c t i", i=RUN, t=PACK)
             if j0 == 0:
                 nc.vector.tensor_copy(out=dst, in_=src)
             else:
                 nc.scalar.copy(out=dst, in_=src)
-            quantize(y_w[:, cols], y_s[:, cols], y_bf[j0][:])
+            quantize(y_w[:, cols], y_s[:, cols], grouped)
             nc.sync.dma_start(out=out_words[:, cols], in_=y_w[:, cols].bitcast(I32))
         for q in range(4):
             queue = nc.scalar if q % 2 else nc.sync

from contextlib import ExitStack

import concourse.mybir as mybir

K, H, N, T, S, K2, T2, R = 1024, 1024, 512, 4096, 1024, 512, 2048, 512
FLOPS = 2 * (K * H * S + H * N * S + K2 * N * R)

F32 = mybir.dt.float32
BF16 = mybir.dt.bfloat16
I32 = mybir.dt.int32
U32 = mybir.dt.uint32
U16 = mybir.dt.uint16
U8 = mybir.dt.uint8
FP8X4 = mybir.dt.float8_e4m3fn_x4
FP4X4 = mybir.dt.float4_e2m1fn_x4
ACT = mybir.ActivationFunctionType
ALU = mybir.AluOpType

P = 128
PACK = 4
KP = P * PACK
RUN = 2
SINES = 16384
TAB1 = 37888
SCALES = 55296
LAST = 11264
EXTRA = 61440
H_GROUPS = [(0, 0, 512, "x"), (0, 512, 512, "x"), (1, 0, 512, "x"), (1, 512, 512, "a")]
Y_CHUNKS = [(0, 384), (384, 128)]


def tile_list_session_tolerance_bound_kernel(
    tc, tab_words, tab_scales, offs, tab2_words, tab2_scales, offs2, pos1, w1, b1, gh, w2_words, w2_scales, w3, tol,
    out_0, out_1, out_2,
):
    nc = tc.nc
    with ExitStack() as ctx:
        keep = ctx.enter_context(tc.tile_pool(name="keep", bufs=1))
        ring = ctx.enter_context(tc.tile_pool(name="ring", bufs=2))
        sring = ctx.enter_context(tc.tile_pool(name="sring", bufs=4))
        shared = ctx.enter_context(tc.tile_pool(name="shared", bufs=1))
        psum = ctx.enter_context(tc.psum_pool(name="psum", bufs=4))

        def held(shape, dtype, name):
            return keep.tile(shape, dtype, name=name, tag=name, align_bytes=64)

        offs_sb = held([P, S // 16], U16, "offs_sb")
        offs2_sb = held([P, R // 16], U16, "offs2_sb")
        pos1_sb = held([P, R // 16], U16, "pos1_sb")
        def placed(shape, dtype, name, offset, tag=None):
            return shared.tile(shape, dtype, name=name, tag=tag or name, align_bytes=64, offset=offset)

        tab_w = [None, None]
        tab_w[0] = placed([P, T], U32, "tab_w0", 0)
        tab_s = placed([P, T], U8, "tab_s", SCALES)
        v_w = [held([P, S], U32, "v_w%d" % a) for a in range(2)]
        w1_raw = {}
        w1_w = {(1, 1): held([P, KP], U32, "w1_w11")}
        w1_s = {(b, a): held([P, KP], U8, "w1_s%d%d" % (b, a)) for b in range(2) for a in range(2)}
        w3_s = held([P, N], U8, "w3_s")
        w2_raw_w = placed([P, 2, 2 * N], U8, "w2_raw_w", TAB1)
        w2_w = held([P, 2, 2 * N], U8, "w2_w")
        b1_sb = held([P, 2, PACK], F32, "b1_sb")
        gh_sb = held([P, 2, PACK], F32, "gh_sb")
        gb_sb = held([P, 2, PACK], F32, "gb_sb")
        tol_sb = held([P, PACK], F32, "tol_sb")
        h_w = [held([P, S], U32, "h_w%d" % b) for b in range(2)]
        h_s = [held([P, S], U8, "h_s%d" % b) for b in range(2)]
        d_sb = [held([P, S], F32, "d_sb%d" % t) for t in range(PACK)]
        y_w = held([P, R], U32, "y_w")
        y_s = held([P, R], U8, "y_s")

        tab2_s = placed([P, T2], U8, "tab2_s", SCALES + 4096)
        w2_raw_s = held([P, 2, N], U8, "w2_raw_s")
        nc.vector.memset(tab_s[:].bitcast(I32), 0)
        nc.vector.memset(tab2_s[:].bitcast(I32), 0)
        nc.vector.memset(w2_raw_s[:].rearrange("p a n -> p (a n)").bitcast(I32), 0)

        def words(ap):
            return ap.rearrange("p n t -> p (n t)").bitcast(I32)

        def load_w1(b, a):
            w1_raw[b, a] = ring.tile([P, PACK, KP], F32, name="w1_raw", tag="raw", align_bytes=64)
            rows = w1[a * KP : (a + 1) * KP, b * KP : (b + 1) * KP]
            nc.sync.dma_start(out=w1_raw[b, a][:], in_=rows.rearrange("(p i) c -> p i c", i=PACK))

        nc.sync.dma_start(offs_sb[:], offs)
        nc.scalar.dma_start(out=b1_sb[:], in_=b1.rearrange("(b p t) -> p b t", b=2, t=PACK))
        nc.scalar.dma_start(out=gh_sb[:], in_=gh.rearrange("(b p t) -> p b t", b=2, t=PACK))
        nc.scalar.dma_start(out=tol_sb[:], in_=tol.rearrange("(p t) -> p t", t=PACK))
        nc.sync.dma_start(out=w2_raw_w[:].bitcast(I32), in_=w2_words.rearrange("a p n -> p a n").bitcast(I32))
        nc.sync.dma_start(out=tab_w[0][:].bitcast(I32), in_=words(tab_words[0]))
        load_w1(0, 0)
        load_w1(0, 1)
        nc.sync.dma_start(offs2_sb[:], offs2)
        nc.sync.dma_start(pos1_sb[:], pos1)
        for q in range(4):
            nc.gpsimd.dma_start(
                out=tab_s[32 * q : 32 * q + 8, :].bitcast(I32), in_=tab_scales[:, 4 * q : 4 * q + 4, :].bitcast(I32)
            )
        for q in range(4):
            nc.gpsimd.dma_start(
                out=tab2_s[32 * q : 32 * q + 4, :].bitcast(I32), in_=tab2_scales[0, 4 * q : 4 * q + 4, :].bitcast(I32)
            )
        for q in range(4):
            nc.gpsimd.dma_start(
                out=w2_raw_s[32 * q : 32 * q + 4, :, :].bitcast(I32),
                in_=w2_scales[:, 4 * q : 4 * q + 4, :].rearrange("a r n -> r a n").bitcast(I32),
            )

        def deal(raw, grouped, scalar_m):
            src = raw[:].rearrange("p i (m t) -> p m i t", t=PACK)
            dst = grouped[:].rearrange("p (t m i) -> p m i t", t=PACK, i=PACK)
            for m0 in range(0, scalar_m, 32):
                nc.scalar.copy(out=dst[:, m0 : m0 + 32], in_=src[:, m0 : m0 + 32])
            if scalar_m < P:
                nc.vector.tensor_copy(out=dst[:, scalar_m:], in_=src[:, scalar_m:])

        def quantize(codes, scales, grouped):
            nc.vector.quantize_mx(out=codes.bitcast(FP8X4), scales=scales, in_=grouped)

        nc.vector.tensor_tensor(out=gb_sb[:], in0=gh_sb[:], in1=b1_sb[:], op=ALU.mult)
        nc.vector.tensor_copy(
            out=w2_w[:].bitcast(U16).rearrange("p a (t m) -> p a m t", t=PACK),
            in_=w2_raw_w[:].bitcast(U16).rearrange("p a (m t) -> p a m t", t=PACK),
        )
        tab_w[1] = placed([P, T], U32, "tab_w1", TAB1)
        nc.sync.dma_start(out=tab_w[1][:].bitcast(I32), in_=words(tab_words[1]))
        nc.vector.tensor_copy(out=v_w[0][:], in_=tab_w[0][:].indirect(offs_sb[:]))
        w1_bf = placed([P, PACK * KP], BF16, "w1_bf00", 0)
        deal(w1_raw[0, 0], w1_bf, P)
        v_s = placed([P, S], U8, "v_s", 8192)
        nc.vector.tensor_copy(out=v_s[:], in_=tab_s[:].indirect(offs_sb[:]))
        w1_w[0, 0] = placed([P, KP], U32, "w1_w00", SCALES)
        quantize(w1_w[0, 0][:], w1_s[0, 0][:], w1_bf[:])
        v2_s = placed([P, R], U8, "v2_s", 0)
        nc.vector.tensor_copy(out=v2_s[:], in_=tab2_s[:].indirect(offs2_sb[:]))
        w1_w[0, 1] = placed([P, KP], U32, "w1_w01", SCALES + 4096)
        w1_bf = placed([P, PACK * KP], BF16, "w1_bf01", 4096)
        deal(w1_raw[0, 1], w1_bf, P)
        quantize(w1_w[0, 1][:], w1_s[0, 1][:], w1_bf[:])
        load_w1(1, 0)
        load_w1(1, 1)
        for half in range(2):
            nc.vector.tensor_copy(
                out=v_w[1][:, 512 * half : 512 * (half + 1)], in_=tab_w[1][:].indirect(offs_sb[:, 32 * half : 32 * (half + 1)])
            )

        w2_s = placed([P, 2, N], U8, "w2_s", TAB1 - 512)
        nc.vector.tensor_copy(
            out=w2_s[:].rearrange("p a (t m) -> p a m t", t=PACK),
            in_=w2_raw_s[:].rearrange("p a (m t) -> p a m t", t=PACK),
        )
        w3_raw = placed([P, PACK, N], F32, "w3_raw", TAB1 + 8704)
        nc.sync.dma_start(out=w3_raw[:], in_=w3.rearrange("(p i) c -> p i c", i=PACK))
        tab2_w = placed([P, T2], U32, "tab2_w", TAB1 + 512)
        nc.sync.dma_start(out=tab2_w[:].bitcast(I32), in_=words(tab2_words[0]))

        def first_stage(g):
            b, j0, n, road = H_GROUPS[g]
            cols = slice(j0, j0 + n)
            if road == "x":
                planes = ring.tile([P, PACK, n], F32, name="planes", tag="planes", align_bytes=64)
            else:
                planes = ring.tile([P, PACK, n], BF16, name="planes", tag="planes", align_bytes=64)
            for t in range(PACK):
                acc = psum.tile([P, n], F32, name="acc", tag="acc")
                m_cols = slice(P * t, P * (t + 1))
                for a in range(2):
                    nc.tensor.matmul_mx(
                        out=acc[:],
                        lhsT=w1_w[b, a][:, m_cols].bitcast(FP8X4),
                        lhsT_scale=w1_s[b, a][:, m_cols],
                        rhs=v_w[a][:, cols].bitcast(FP8X4),
                        rhs_scale=v_s[4 * a :, cols],
                        start=(a == 0),
                        stop=(a == 1),
                    )
                if g == 2:
                    sine = placed([P, n], F32, "sine_third%d" % t, EXTRA + 2048 * t)
                else:
                    slot = PACK * (g == 1) + t
                    sine = placed([P, n], F32, "sine%d" % slot, SINES + 2048 * slot)
                nc.scalar.activation(out=sine[:], in_=acc[:], func=ACT.Sin, bias=b1_sb[:, b, t : t + 1])
                if road == "x":
                    nc.vector.scalar_tensor_tensor(
                        out=planes[:, t, :], in0=acc[:], scalar=b1_sb[:, b, t : t + 1], in1=sine[:], op0=ALU.add, op1=ALU.add
                    )
                else:
                    gained = sring.tile([P, n], F32, name="gained", tag="gained")
                    nc.scalar.activation(
                        out=gained[:], in_=acc[:], func=ACT.Identity, bias=gb_sb[:, b, t : t + 1], scale=gh_sb[:, b, t : t + 1]
                    )
                    nc.vector.scalar_tensor_tensor(
                        out=planes[:, t, :], in0=sine[:], scalar=gh_sb[:, b, t : t + 1], in1=gained[:], op0=ALU.mult, op1=ALU.add
                    )
            return planes

        def finish_h(g, planes):
            b, j0, n, road = H_GROUPS[g]
            if g == len(H_GROUPS) - 1:
                grouped = placed([P, n * PACK], BF16, "h_bf_last", LAST)
            elif g == 1:
                grouped = placed([P, n * PACK], BF16, "h_bf_second", SINES + 4096)
            else:
                grouped = ring.tile([P, n * PACK], BF16, name="h_bf", tag="h_bf", align_bytes=64)
            run = 2 if road == "x" else 4
            src = planes[:].rearrange("p t (c i) -> p c t i", i=run)
            dst = grouped[:].rearrange("p (c i t) -> p c t i", i=run, t=PACK)
            if road == "x":
                gain = gh_sb[:, b, :].unsqueeze(1).unsqueeze(3).broadcast_to([P, n // run, PACK, run])
                nc.vector.tensor_tensor(out=dst, in0=src, in1=gain, op=ALU.mult)
            else:
                nc.vector.tensor_copy(out=dst, in_=src)
            quantize(h_w[b][:, j0 : j0 + n], h_s[b][:, j0 : j0 + n], grouped[:])

        def second_stage(groups):
            first = H_GROUPS[groups[0]][1]
            for t in range(PACK):
                dacc = psum.tile([P, KP], F32, name="dacc", tag="dacc")
                for g in groups:
                    j0, n = H_GROUPS[g][1:3]
                    cols = slice(j0, j0 + n)
                    for b in range(2):
                        nc.tensor.matmul_mx(
                            out=dacc[:, j0 - first : j0 - first + n],
                            lhsT=w2_w[:, b, 2 * P * t : 2 * P * (t + 1)].bitcast(FP4X4),
                            lhsT_scale=w2_s[:, b, P * t : P * (t + 1)],
                            rhs=h_w[b][:, cols].bitcast(FP8X4),
                            rhs_scale=h_s[b][:, cols],
                            start=(b == 0),
                            stop=(b == 1),
                        )
                nc.scalar.copy(out=d_sb[t][:, first : first + KP], in_=dacc[:])

        planes = first_stage(0)
        finish_h(0, planes)
        planes = first_stage(1)
        w1_bf10 = placed([P, PACK * KP], BF16, "w1_bf10", SINES)
        deal(w1_raw[1, 0], w1_bf10, P)
        w1_bf11 = placed([P, PACK * KP], BF16, "w1_bf11", SINES + 4096)
        deal(w1_raw[1, 1], w1_bf11, 64)
        w1_w[1, 0] = placed([P, KP], U32, "w1_w10", SINES + 2048 * 7)
        quantize(w1_w[1, 0][:], w1_s[1, 0][:], w1_bf10[:])
        quantize(w1_w[1, 1][:], w1_s[1, 1][:], w1_bf11[:])
        finish_h(1, planes)
        planes = first_stage(2)
        w3_bf = placed([P, PACK * N], BF16, "w3_bf", SINES + 8192)
        deal(w3_raw, w3_bf, P)
        finish_h(2, planes)
        for g in range(3, len(H_GROUPS)):
            finish_h(g, first_stage(g))
        second_stage([2])
        second_stage([3])

        v2_w = placed([P, R], U32, "v2_w", LAST - 1024)
        nc.vector.tensor_copy(out=v2_w[:], in_=tab2_w[:].indirect(offs2_sb[:]))
        w3_w = placed([P, N], U32, "w3_w", LAST + 1024)
        quantize(w3_w[:], w3_s[:], w3_bf[:])
        b_acc = []
        for t in range(PACK):
            acc = psum.tile([P, R], F32, name="acc", tag="acc")
            m_cols = slice(P * t, P * (t + 1))
            nc.tensor.matmul_mx(
                out=acc[:],
                lhsT=w3_w[:, m_cols].bitcast(FP8X4),
                lhsT_scale=w3_s[:, m_cols],
                rhs=v2_w[:].bitcast(FP8X4),
                rhs_scale=v2_s[:],
                start=True,
                stop=True,
            )
            b_acc.append(acc)

        out_rows = out_0.rearrange("(p t) j -> p t j", t=PACK)
        out_words = words(out_1[0])
        y = held([P, PACK, R], F32, "y")
        y_bf = held([P, PACK * R], BF16, "y_bf")

        def pick(t, j0, n):
            picked = ring.tile([P, n], F32, name="picked", tag="picked")
            nc.vector.tensor_copy(out=picked[:], in_=d_sb[t][:].indirect(pos1_sb[:, j0 // 16 : (j0 + n) // 16]))
            return picked

        def bound(t, j0, n, picked):
            cols = slice(j0, j0 + n)
            lower = sring.tile([P, n], F32, name="lower", tag="gained")
            nc.vector.tensor_tensor(out=lower[:], in0=picked[:], in1=b_acc[t][:, cols], op=ALU.min)
            nc.scalar.activation(out=y[:, t, cols], in_=lower[:], func=ACT.Copy, scale=tol_sb[:, t : t + 1])
            nc.sync.dma_start(out=out_rows[:, t, cols], in_=y[:, t, cols])

        pieces = [(t, 0, R) for t in range(PACK - 1)] + [(PACK - 1, j0, n) for j0, n in Y_CHUNKS]
        ahead = pick(*pieces[0])
        for piece, following in zip(pieces, pieces[1:] + [None]):
            picked = ahead
            if following is not None:
                ahead = pick(*following)
            bound(*piece, picked)
        for j0, n in Y_CHUNKS:
            cols = slice(j0, j0 + n)
            grouped = y_bf[:, PACK * j0 : PACK * (j0 + n)]
            src = y[:, :, cols].rearrange("p t (c i) -> p c t i", i=RUN)
            dst = grouped.rearrange("p (c i t) -> p c t i", i=RUN, t=PACK)
            if j0 == 0:
                nc.vector.tensor_copy(out=dst, in_=src)
            else:
                nc.scalar.copy(out=dst, in_=src)
            quantize(y_w[:, cols], y_s[:, cols], grouped)
            nc.sync.dma_start(out=out_words[:, cols], in_=y_w[:, cols].bitcast(I32))
        for q in range(4):
            queue = nc.scalar if q % 2 else nc.sync
            queue.dma_start(out=out_2[0, 4 * q : 4 * q + 4, :].bitcast(I32), in_=y_s[32 * q : 32 * q + 4, :].bitcast(I32))
